import numpy as np, ml_dtypes
CORES = [66,74,82,90,194,202,210,218]
N = 8
import mx_ref
BF = ml_dtypes.bfloat16
def entries(a):
    return np.ascontiguousarray(a.T).reshape(-1)
def table(e):
    return np.ascontiguousarray(np.reshape(e, (-1, 16)).T).astype(np.int32)
def cols(t, e):
    v = np.concatenate([t.reshape(128, -1, 4), np.zeros((128, 1, 4), BF)], axis=1)
    return np.ascontiguousarray(v[:, e]).reshape(128, -1)
def tile(rs):
    return np.stack(rs, axis=2).reshape(128, -1).astype(BF)
def cut(t, i, w=512):
    return t[:, w * i:w * i + w]
def f(rng, *shape):
    return mx_ref.flush((rng.standard_normal(shape, dtype=np.float32) * np.exp2(rng.integers(-2, 3, shape[:-1] + (1,)))).astype(BF))
def wide(rng, *shape, cols=0):
    v = rng.standard_normal(shape, dtype=np.float32) * np.exp2(rng.integers(-12, 13, shape)).astype(np.float32)
    if cols: v *= np.repeat(np.exp2(rng.integers(-cols, cols + 1, shape[:-2] + (1, shape[-1] // 4))) * (rng.random(shape[:-2] + (1, shape[-1] // 4)) > 0.0625), 4, axis=-1).astype(np.float32)
    return mx_ref.flush(v.astype(BF))
S, C1, C2 = 128, 16, 24
def pack(nb):
    return {"nb0": np.stack([table(e) for e in nb[0].reshape(N, S)]), "nb1": np.stack([table(e) for e in nb[1].reshape(N, S)])}
def lists(rng):
    pool = [[(q * S + rng.permutation(S)[:rng.integers(1, 3 * C1 // 4 + 1)]).tolist() for q in range(N)] for r in range(N)]
    skew = []
    for r in range(N):
        p = np.exp2(rng.integers(0, 4, N)).astype(float); p[r] = 0
        skew.append(np.divide(p, p.sum()))
    who = {n: [] for n in range(N * S)}
    near, hand = {}, {}
    for r in range(N):
        for q in range(N):
            if q == r: continue
            for n in pool[r][q]: who[n].append(r)
            near[r, q] = set(pool[r][q]); hand[r, q] = set(pool[r][q])
    def one(r):
        if rng.random() < 0.6: return int(r * S + rng.integers(0, S))
        p = pool[r][int(rng.choice(N, p=skew[r]))]
        return p[rng.integers(0, len(p))]
    def fits(n, w):
        return all((w // S == r or len(near[r, w // S] | {w}) <= C2) and len(hand[r, n // S] | {w}) <= C2 for r in who[n])
    nb = np.zeros((2, N * S), int)
    for n in rng.permutation(N * S).tolist():
        for k in range(2):
            for _ in range(8):
                w = one(n // S)
                if fits(n, w): break
            else: w = n
            nb[k, n] = w
            for r in who[n]:
                if w // S != r: near[r, w // S].add(w)
                hand[r, n // S].add(w)
    for r in range(N):
        free = rng.permutation([n for n in range(r * S, r * S + S) if not who[n]])
        nb[1, free[:S // 20]] = nb[0, free[:S // 20]]
        for k in range(2):
            p = rng.permutation(free)[:2 * (S >> 6)]
            nb[k, p] = p[::-1]
    return pack(nb)
def weights(rng, n):
    return np.stack([f(rng, 128, 512 * n)] * N)
def setup_inputs(rng):
    return {"x": f(rng, N, 128, 4 * S), "a": weights(rng, 8), "v": weights(rng, 2), "u": weights(rng, 2), **lists(rng)}
def setup_inputs_apart(rng):
    d = setup_inputs(rng)
    nb = np.zeros((2, N * S), int)
    e, m = C2 - C1, S - (N - 1) * C1
    h = min(-(-m // (N - 1)), e - 2)
    p = [q * S + rng.permutation(S) for q in range(N)]
    F, H = {}, {}
    for q in range(N):
        for i in range(N - 1):
            r = (q + 1 + i) % N
            F[r, q] = p[q][C1 * i:C1 * i + C1]
            H[r, q] = p[q][(N - 1) * C1 + (h * i + np.arange(h)) % m]
    for r, q in F:
        s = (q + 1) % N
        if s == r: s = (q + 2) % N
        D = np.concatenate([H[r, q], rng.permutation(F[q, s])[:e - h]])
        k = (r + q) % 2
        nb[k, F[r, q]] = rng.permutation(F[q, r])
        nb[1 - k, F[r, q]] = np.concatenate([rng.permutation(D), F[q, r][:C1 - e]])
    for r in range(N):
        rest = p[r][(N - 1) * C1:]
        far = np.concatenate([F[r, q] for q in range(N) if q != r])
        for k in range(2):
            must = [int(n) for q in range(N) if q != r and (r + q) % 2 != k for n in F[r, q][C1 - e:e]]
            nb[k, rest] = rng.permutation(must + rng.choice(np.concatenate([far, p[r]]), m - len(must)).tolist())
    return {**d, **pack(nb)}
def setup_inputs_full(rng):
    d = setup_inputs(rng)
    nb = np.zeros((2, N * S), int)
    p = [q * S + rng.permutation(S) for q in range(N)]
    B = [e[:C1] for e in p]
    for q in range(N):
        some = rng.permutation(np.concatenate(B))[:C1]
        nb[:, B[q]] = rng.permutation(np.concatenate([p[q][C1:C2], some, rng.choice(some, 2 * C1 - C2)])).reshape(2, C1)
        rest = p[q][C1:]
        far = np.concatenate([B[s] for s in range(N) if s != q])
        for k in range(2):
            nb[k, rest] = rng.permutation(np.concatenate([far, rng.choice(np.concatenate([far, p[q]]), len(rest) - len(far))]))
    return {**d, **pack(nb)}
def setup_inputs_hub(rng):
    d = setup_inputs(rng)
    nb = np.zeros((2, N * S), int)
    for r in range(N):
        for k in range(2): nb[k, r * S:r * S + S] = (r + rng.integers(1, N)) % N * S + rng.integers(0, S)
    return {**d, **pack(nb)}
def setup_inputs_spread(rng):
    d = setup_inputs(rng); d["x"] = wide(rng, N, 128, 4 * S); return d
def setup_inputs_most(rng):
    d = setup_inputs(rng)
    nb = np.zeros((2, N * S), int)
    p = [q * S + rng.permutation(S) for q in range(N)]
    B = [e[:C1] for e in p]
    for q in range(N):
        nb[:, B[q]] = rng.permutation(np.concatenate([p[q][:C2], rng.choice(p[q][:C2], 2 * C1 - C2)])).reshape(2, C1)
        far = np.concatenate([B[s] for s in range(N) if s != q])
        must = np.concatenate([far, p[q][C2:]])
        nb[:, p[q][C1:]] = rng.permutation(np.concatenate([must, rng.choice(np.concatenate([far, p[q]]), 2 * (S - C1) - len(must))])).reshape(2, S - C1)
    return {**d, **pack(nb)}
def check_inputs(d):
    b = []
    nb = np.stack([np.concatenate([entries(e) for e in d[n]]) for n in ("nb0", "nb1")])
    for n in ("a", "v", "u"):
        if (d[n] != d[n][:1]).any(): b.append(n + " isn't the same on all ranks")
    if nb.min() < 0 or nb.max() >= N * S: return b + ["nb0, nb1"]
    for r in range(N):
        own = nb[:, r * S:r * S + S]
        first = np.unique(own)
        near = np.unique(np.concatenate([first, nb[0][first], nb[1][first]]))
        for q in range(N):
            if q == r: continue
            if (first // S == q).sum() > C1: b.append("too many neighbours on one other rank")
            if (near // S == q).sum() > C2: b.append("too many nodes of one other rank in two steps")
            behind = np.concatenate([nb[k][own[k][own[k] // S == q]] for k in range(2)])
            if len(np.unique(behind)) > C2: b.append("too many nodes behind neighbours on one other rank")
    return b
def product(w, t, e):
    n, i = np.unique(e, return_inverse=True)
    n = np.concatenate([n, np.full(-len(n) % 16, n[0])])
    return mx_ref.matmul(mx_ref.quantize(np.ascontiguousarray(w)), mx_ref.quantize(cols(t, n)))[:, i.reshape(-1)]
def reference(x, a, v, u, nb0, nb1):
    nb = np.stack([np.concatenate([entries(e) for e in n]) for n in (nb0, nb1)])
    x = np.concatenate(list(x), axis=1)
    named = np.unique(nb)
    R = []
    for b in range(4):
        P = product(cut(a[0], b), x, nb[0][named]) + product(cut(a[0], 4 + b), x, nb[1][named])
        R.append(np.maximum(P, np.float32(0)) * np.float32(0.05))
    h = np.zeros((128, N * S, 4), BF)
    h[:, named] = tile(R).reshape(128, -1, 4)
    h = h.reshape(128, -1)
    y = product(cut(v[0], 0), h, nb[0]) + product(cut(v[0], 1), h, nb[1]) + product(cut(u[0], 0), x, nb[0][nb[0]]) + product(cut(u[0], 1), x, nb[1][nb[1]])
    return {"y": np.stack([y[:, r * S:r * S + S] for r in range(N)])}

@@ -1,0 +1,290 @@
+from concourse.bass import DstId, RemoteDMATransfer
+from concourse.mybir import dt, AluOpType as Op, ActivationFunctionType as Act
+
+CODE = "float8_e4m3fn_x4"
+
+
+def _sb(n, d):
+    return ("sbuf", [128, n], d)
+
+
+SCRATCH = {
+    "L32": _sb(16, "int32"), "Loff": _sb(16, "uint16"), "Ldup": _sb(32, "uint16"),
+    "pid": _sb(1, "int32"), "grp": _sb(1, "int32"), "e0": _sb(1, "int32"), "e1": _sb(1, "int32"),
+    "lane": _sb(1, "int32"), "lanef": _sb(1, "float32"), "g128": _sb(1, "float32"), "base": _sb(1, "float32"),
+    "j16": _sb(8, "int32"), "jcol": _sb(8, "float32"), "st": _sb(16, "int32"), "Soff": _sb(16, "uint16"),
+    "iw": _sb(1024, "float32"), "W01": _sb(16, "bfloat16"),
+    "Lf": _sb(256, "bfloat16"), "eq": _sb(2048, "bfloat16"), "sc": _sb(1024, "bfloat16"), "moff": _sb(8, "uint16"),
+    "mk": _sb(128, "bfloat16"), "cum": _sb(128, "bfloat16"), "le": _sb(128, "bfloat16"), "fs": _sb(64, "bfloat16"),
+    "Fmsg": _sb(1, "uint16"), "Fland": _sb(7, "uint16"), "Frep": _sb(8, "uint16"), "Fdup": _sb(14, "uint16"),
+    "tabv": _sb(128, "bfloat16"), "tab": _sb(1024, "bfloat16"),
+    "P1f": _sb(512, "bfloat16"), "P1t": _sb(512, "bfloat16"), "P1off": _sb(16, "uint16"), "P1n": _sb(256, "bfloat16"),
+    "L2f": _sb(448, "bfloat16"), "L2t": _sb(448, "bfloat16"), "L2off": _sb(14, "uint16"),
+    "xt": _sb(512, "bfloat16"), "at": _sb(4096, "bfloat16"), "vt": _sb(1024, "bfloat16"), "ut": _sb(1024, "bfloat16"),
+    "ht": _sb(960, "bfloat16"), "yt": _sb(128, "float32"),
+    "psE": ("psum", [128, 1536], "float32"), "psL": ("psum", [128, 1536], "float32"),
+    "ps3": ("psum", [128, 512], "float32"), "psY": ("psum", [128, 512], "float32"),
+}
+for _n, _w in (("A", 1024), ("V", 256), ("U", 256), ("x0", 128), ("W1", 240), ("s1", 112), ("s2", 224), ("L2", 224),
+               ("M0", 240), ("M1", 240), ("um0", 128), ("um1", 128), ("H", 240), ("vm0", 128), ("vm1", 128)):
+    SCRATCH[_n + "q"] = _sb(_w, CODE)
+    SCRATCH[_n + "s"] = _sb(_w, "uint8")
+
+SEMAPHORES = ["vs", "as_", "ts", "gs", "dl", "dx", "da", "dv", "du", "dt_", "df", "dy",
+              "arr1", "arr2c", "arr2s", "arr3c", "arr3s", "loc"]
+
+
+def rank_program(g, core, T, topo):
+    rank = T.rank_of(core)
+    if rank is None:
+        return
+    N = len(T.cores)
+    S = 128
+    vec, act, ten, syn = g.vector, g.scalar, g.tensor, g.sync
+    queues = {"g": g, "v": vec, "a": act, "t": ten, "s": syn}
+    cnt, seen = {}, {}
+
+    def inc(ins, s, n=1):
+        ins.then_inc(T.sem[s], n)
+        cnt[s] = cnt.get(s, 0) + n
+        return (s, cnt[s])
+
+    def need(q, *toks):
+        for s, n in toks:
+            if seen.get((q, s), 0) < n:
+                queues[q].wait_ge(T.sem[s], n)
+                seen[(q, s)] = n
+
+    def V(ins):
+        return inc(ins, "vs")
+
+    def A(ins):
+        return inc(ins, "as_")
+
+    def G(ins):
+        return inc(ins, "gs")
+
+    def D(q, s, out, in_):
+        return inc(queues[q].dma_start(out, in_), s, 16)
+
+    def exchange(src, dst, width, base, sem, turn, codes):
+        ts = []
+        for d in range(1, N):
+            to = T.cores[(rank + d) % N]
+            rid, pnc = topo.addr(to, core)
+            eng = topo.engines(core, to)
+            a = (d - 1) * width
+            b = base + (N - d - 1) * width
+            s_, d_ = T[src][:, a:a + width], T[dst][:, b:b + width]
+            if codes:
+                s_, d_ = s_.bitcast(dt.uint8), d_.bitcast(dt.uint8)
+            ts.append(RemoteDMATransfer(dst_ids=[DstId(rid=rid, pnc=pnc)], dma_engine_mask=1 << eng[(d - 1 + turn) % len(eng)],
+                                        remote_sem=T.sem[sem], src=s_, dst=d_))
+        g.remote_dma_fused(ts, local_sem=T.sem.loc)
+        cnt["loc"] = cnt.get("loc", 0) + N - 1
+        cnt[sem] = N - 1
+
+    for k in range(8):
+        rows = slice(16 * k, 16 * k + 16)
+        D("s", "dl", T.L32[rows, 0:8], T.nb0[:])
+        t_dl = D("a", "dl", T.L32[rows, 8:16], T.nb1[:])
+    t_dx = D("s", "dx", T.xt[:], T.x[:])
+    D("a", "da", T.at[:, 0:2048], T.a[:, 0:2048])
+    t_da = D("s", "da", T.at[:, 2048:4096], T.a[:, 2048:4096])
+    t_du = D("a", "du", T.ut[:], T.u[:])
+    t_dv = D("s", "dv", T.vt[:], T.v[:])
+
+    t_pid = G(g.iota(T.pid[:], [[0, 1]], 0, 1))
+    t_iw = G(g.iota(T.iw[:, 0:512], [[1, 512]], 0, 0, allow_small_or_imprecise_dtypes=True))
+    t_j16 = G(g.iota(T.j16[:], [[16, 8]], 0, 0))
+    t_w01 = G(g.iota(T.W01[:], [[1, 16]], 0, 0, allow_small_or_imprecise_dtypes=True))
+    t_st = G(g.iota(T.st[:], [[16, 2], [32, 8]], 0, 0))
+    t_tab0 = V(vec.memset(T.tab[:], 0.0))
+    need("v", t_pid)
+    t_grp = V(vec.tensor_scalar(T.grp[:], T.pid[:], 4, None, Op.arith_shift_right))
+    t_lane = V(vec.tensor_scalar(T.lane[:], T.pid[:], 15, None, Op.bitwise_and))
+    need("v", t_grp)
+    t_g128 = V(vec.tensor_scalar(T.g128[:], T.grp[:], 128.0, None, Op.mult))
+    t_e0 = V(vec.tensor_scalar(T.e0[:], T.grp[:], float(N - rank), None, Op.add))
+    need("v", t_lane)
+    t_lanef = V(vec.tensor_copy(T.lanef[:], T.lane[:]))
+    need("v", t_e0)
+    t_e1 = V(vec.tensor_scalar(T.e1[:], T.e0[:], N - 1, None, Op.bitwise_and))
+    need("v", t_e1)
+    t_base = V(vec.tensor_scalar(T.base[:], T.e1[:], 16.0, float(S - 16 - 1), Op.mult, Op.add))
+    need("v", t_iw)
+    t_iw2 = V(vec.tensor_scalar(T.iw[:, 512:1024], T.iw[:, 0:512], 512.0, None, Op.add))
+    need("v", t_j16, t_lanef)
+    t_jcol = V(vec.tensor_scalar(T.jcol[:], T.j16[:], T.lanef[:, 0:1], None, Op.add))
+    need("v", t_tab0)
+    t_own = V(vec.tensor_copy(T.tab[:, S * rank:S * rank + S], T.iw[:, 0:S]))
+
+    need("v", t_dl)
+    t_loff = V(vec.tensor_copy(T.Loff[:], T.L32[:]))
+    need("v", t_loff, t_iw2, t_g128)
+    t_lf = V(vec.tensor_scalar(T.Lf[:], T.iw[:].indirect(T.Loff[:]), T.g128[:, 0:1], None, Op.subtract))
+    need("v", t_lf, t_jcol)
+    t_eq = [V(vec.tensor_scalar(T.eq[:, 256 * t:256 * t + 256], T.Lf[:], T.jcol[:, t:t + 1], None, Op.is_equal)) for t in range(8)]
+    for t in range(8):
+        need("v", t_eq[t])
+        t_sc = V(vec.tensor_tensor_scan(T.sc[:, 128 * t:128 * t + 128], T.eq[:, 256 * t:256 * t + 128],
+                                        T.eq[:, 256 * t + 128:256 * t + 256], 0.0, Op.max, Op.max))
+    need("v", t_sc)
+    t_moff = V(vec.tensor_copy(T.moff[:], T.sc[:, 127:1024:128]))
+    need("v", t_moff, t_w01)
+    t_mk = V(vec.tensor_copy(T.mk[:], T.W01[:].indirect(T.moff[:])))
+    need("v", t_mk)
+    t_cum = V(vec.tensor_tensor_scan(T.cum[:], T.mk[:], T.mk[:], 0.0, Op.add, Op.max))
+    need("v", t_cum)
+    t_le = V(vec.tensor_scalar(T.le[:], T.cum[:], T.lanef[:, 0:1], None, Op.is_le))
+    need("v", t_le)
+    t_fs = V(vec.tensor_tensor_scan(T.fs[:], T.le[:, 0:64], T.le[:, 64:128], 0.0, Op.add, Op.add))
+    need("v", t_fs)
+    t_f = V(vec.tensor_scalar(T.Fmsg[:], T.fs[:, 63:64], float(S - 1), None, Op.min))
+
+    need("g", t_f)
+    ts = []
+    for d in range(1, N):
+        to = T.cores[(rank + d) % N]
+        rid, pnc = topo.addr(to, core)
+        eng = topo.engines(core, to)
+        ts.append(RemoteDMATransfer(dst_ids=[DstId(rid=rid, pnc=pnc)], dma_engine_mask=1 << eng[(d - 1) % len(eng)],
+                                    remote_sem=T.sem.arr1, src=T.Fmsg[:], dst=T.Fland[:, N - 1 - d:N - d]))
+    g.remote_dma_fused(ts, local_sem=T.sem.loc)
+    cnt["loc"] = N - 1
+    cnt["arr1"] = N - 1
+
+    t_tabv = V(vec.tensor_scalar(T.tabv[:], T.cum[:], T.base[:, 0:1], None, Op.add))
+    for n, d in enumerate(range(1, N)):
+        q = "sa"[n % 2]
+        k = (rank + d) % N
+        need(q, t_tabv, t_own)
+        t_tab = D(q, "dt_", T.tab[0:128:32, S * k:S * k + S], T.tabv[16 * k:16 * k + 4, :])
+    V(vec.tensor_copy(T.Ldup[:, 0:32:2], T.L32[:]))
+    t_ldup = V(vec.tensor_copy(T.Ldup[:, 1:32:2], T.L32[:]))
+    need("v", t_st)
+    t_soff = V(vec.tensor_scalar(T.Soff[:], T.st[:], T.lanef[:, 0:1], None, Op.add))
+    need("v", t_dx)
+    t_x0 = V(vec.quantize_mx(T.x0q[:], T.x0s[:], T.xt[:]))
+    t_w1 = V(vec.quantize_mx(T.W1q[:, 0:S], T.W1s[:, 0:S], T.xt[:]))
+    need("v", t_tab, t_ldup)
+    t_p1f = V(vec.tensor_copy(T.P1f[:], T.tab[:].indirect(T.Ldup[:])))
+    t_p1n = V(vec.tensor_copy(T.P1n[:], T.tab[:].indirect(T.Loff[:])))
+    need("v", t_p1f)
+    t_p1t = V(vec.transpose(T.P1t[:], T.P1f[:]))
+    need("v", t_p1t)
+    t_p1 = V(vec.tensor_copy(T.P1off[:], T.P1t[:, 0:512:32]))
+
+    for k in range(8):
+        q = "sa"[k % 2]
+        need(q, ("arr1", N - 1))
+        t_frep = D(q, "df", T.Frep[16 * k:16 * k + 16, 0:7], T.Fland[16 * rank:16 * rank + 16, 0:7])
+    need("v", t_frep, t_x0)
+    t_s1q = V(vec.tensor_copy(T.s1q[:].bitcast(dt.uint32), T.x0q[:].bitcast(dt.uint32).indirect(T.Frep[:, 0:7])))
+    need("a", t_frep, t_x0)
+    t_s1s = A(act.activation(T.s1s[:], T.x0s[:].indirect(T.Frep[:, 0:7]), Act.Copy))
+    need("g", t_s1q)
+    exchange("s1q", "W1q", 16, S, "arr2c", 0, True)
+    need("g", t_s1s)
+    exchange("s1s", "W1s", 16, S, "arr2s", N - 1, False)
+
+    V(vec.tensor_copy(T.Fdup[:, 0:14:2], T.Frep[:, 0:7]))
+    t_fdup = V(vec.tensor_copy(T.Fdup[:, 1:14:2], T.Frep[:, 0:7]))
+    need("v", t_fdup, t_p1n)
+    V(vec.tensor_copy(T.L2f[:, 0:224], T.P1n[:, 0:S].indirect(T.Fdup[:])))
+    t_l2f = V(vec.tensor_copy(T.L2f[:, 224:448], T.P1n[:, S:2 * S].indirect(T.Fdup[:])))
+    need("v", t_l2f)
+    t_l2t = V(vec.transpose(T.L2t[:], T.L2f[:]))
+    need("v", t_l2t)
+    V(vec.tensor_copy(T.L2off[:, 0:14:2], T.L2t[:, 0:224:32]))
+    t_l2 = V(vec.tensor_copy(T.L2off[:, 1:14:2], T.L2t[:, 224:448:32]))
+    need("v", t_da)
+    V(vec.quantize_mx(T.Aq[:, 0:512], T.As[:, 0:512], T.at[:, 0:2048]))
+    t_aq = V(vec.quantize_mx(T.Aq[:, 512:1024], T.As[:, 512:1024], T.at[:, 2048:4096]))
+    need("v", t_du, t_dv)
+    t_uq = V(vec.quantize_mx(T.Uq[:], T.Us[:], T.ut[:]))
+    t_vq = V(vec.quantize_mx(T.Vq[:], T.Vs[:], T.vt[:]))
+
+    need("v", ("arr2c", N - 1), t_l2, t_w1)
+    t_s2q = V(vec.tensor_copy(T.s2q[:].bitcast(dt.uint32), T.W1q[:].bitcast(dt.uint32).indirect(T.L2off[:])))
+    need("a", ("arr2s", N - 1), t_l2, t_w1)
+    t_s2s = A(act.activation(T.s2s[:], T.W1s[:].indirect(T.L2off[:]), Act.Copy))
+    need("g", t_s2q)
+    exchange("s2q", "L2q", 32, 0, "arr3c", 0, True)
+    need("g", t_s2s)
+    exchange("s2s", "L2s", 32, 0, "arr3s", N - 1, False)
+
+    need("v", t_p1)
+    need("a", t_p1)
+    own_c, own_s = [], []
+    for k in range(2):
+        off = T.P1off[:, 8 * k:8 * k + 8]
+        own_c.append(V(vec.tensor_copy(T["M%dq" % k][:, 0:S].bitcast(dt.uint32), T.W1q[:].bitcast(dt.uint32).indirect(off))))
+        own_s.append(A(act.activation(T["M%ds" % k][:, 0:S], T.W1s[:].indirect(off), Act.Copy)))
+
+    def products(ps, b, lo, hi):
+        for k in range(2):
+            w = slice(128 * (4 * k + b), 128 * (4 * k + b) + 128)
+            ins = ten.matmul_mx(ps, T.Aq[:, w], T.As[:, w], T["M%dq" % k][:, lo:hi], T["M%ds" % k][:, lo:hi], k == 0, k == 1)
+        return inc(ins, "ts")
+
+    def relu(q, out, ps, tok):
+        need(q, tok)
+        if q == "v":
+            return V(vec.tensor_scalar(out, ps, 0.0, 0.05, Op.max, Op.mult))
+        return A(act.activation(out, ps, Act.Relu, scale=0.05))
+
+    need("t", t_aq, *own_c, *own_s)
+    early = [products(T.psE[:, 512 * b:512 * b + S], b, 0, S) for b in range(3)]
+    hb = []
+    for b in range(3):
+        hb.append(relu("ava"[b], T.ht[:, b:512:4], T.psE[:, 512 * b:512 * b + S], early[b]))
+
+    rem_c, rem_s = [], []
+    need("v", ("arr3c", N - 1), t_soff)
+    need("a", ("arr3s", N - 1), t_soff)
+    for k in range(2):
+        off = T.Soff[:, 8 * k:8 * k + 7]
+        rem_c.append(V(vec.tensor_copy(T["M%dq" % k][:, S:240].bitcast(dt.uint32), T.L2q[:].bitcast(dt.uint32).indirect(off))))
+        rem_s.append(A(act.activation(T["M%ds" % k][:, S:240], T.L2s[:].indirect(off), Act.Copy)))
+    need("t", *rem_c, *rem_s)
+    late3 = products(T.ps3[:, 0:240], 3, 0, 240)
+    late = [products(T.psL[:, 512 * b:512 * b + S], b, 112, 240) for b in range(3)]
+
+    um_c, um_s = [], []
+    need("v", *rem_c)
+    need("a", *rem_s)
+    for k in range(2):
+        off = T.P1off[:, 8 * k:8 * k + 8]
+        um_c.append(V(vec.tensor_copy(T["um%dq" % k][:].bitcast(dt.uint32), T["M%dq" % k][:].bitcast(dt.uint32).indirect(off))))
+        um_s.append(A(act.activation(T["um%ds" % k][:], T["M%ds" % k][:].indirect(off), Act.Copy)))
+
+    h3 = relu("a", T.ht[:, 3:960:4], T.ps3[:, 0:240], late3)
+    h0 = relu("v", T.ht[:, 512:960:4], T.psL[:, 16:S], late[0])
+    h1 = relu("a", T.ht[:, 513:960:4], T.psL[:, 512 + 16:512 + S], late[1])
+    need("v", h3, *hb)
+    t_h_own = V(vec.quantize_mx(T.Hq[:, 0:S], T.Hs[:, 0:S], T.ht[:, 0:512]))
+    h2 = relu("v", T.ht[:, 514:960:4], T.psL[:, 1024 + 16:1024 + S], late[2])
+    need("v", t_h_own, h0, h1, h2)
+    t_h = V(vec.quantize_mx(T.Hq[:, 112:240], T.Hs[:, 112:240], T.ht[:, 448:960]))
+    need("v", t_h)
+    need("a", t_h)
+    vm_c, vm_s = [], []
+    for k in range(2):
+        off = T.P1off[:, 8 * k:8 * k + 8]
+        vm_c.append(V(vec.tensor_copy(T["vm%dq" % k][:].bitcast(dt.uint32), T.Hq[:].bitcast(dt.uint32).indirect(off))))
+        vm_s.append(A(act.activation(T["vm%ds" % k][:], T.Hs[:].indirect(off), Act.Copy)))
+
+    steps = [("U", "um", 0, um_c, um_s, t_uq), ("U", "um", 1, um_c, um_s, t_uq), ("V", "vm", 0, vm_c, vm_s, t_vq), ("V", "vm", 1, vm_c, vm_s, t_vq)]
+    for n, (w, m, k, c_, s_, t_) in enumerate(steps):
+        need("t", t_, c_[k], s_[k])
+        ks = slice(128 * k, 128 * k + 128)
+        ins = ten.matmul_mx(T.psY[:, 0:S], T[w + "q"][:, ks], T[w + "s"][:, ks], T["%s%dq" % (m, k)][:], T["%s%ds" % (m, k)][:], n == 0, n == 3)
+    t_y = inc(ins, "ts")
+    need("v", t_y)
+    t_yt = V(vec.tensor_copy(T.yt[:], T.psY[:, 0:S]))
+    need("s", t_yt)
+    D("s", "dy", T.y[:], T.yt[:])
+
+    for s in SEMAPHORES:
+        need("g", (s, cnt[s]))

@@ -11,9 +11,9 @@ def _sb(n, d):
 SCRATCH = {
     "L32": _sb(16, "int32"), "Loff": _sb(16, "uint16"), "Ldup": _sb(32, "uint16"),
     "pid": _sb(1, "int32"), "grp": _sb(1, "int32"), "e0": _sb(1, "int32"), "e1": _sb(1, "int32"),
-    "lane": _sb(1, "int32"), "lanef": _sb(1, "float32"), "g128": _sb(1, "float32"), "base": _sb(1, "float32"),
-    "j16": _sb(8, "int32"), "jcol": _sb(8, "float32"), "st": _sb(16, "int32"), "Soff": _sb(16, "uint16"),
-    "iw": _sb(1024, "float32"), "W01": _sb(16, "bfloat16"),
+    "lane": _sb(1, "int32"), "lanef": _sb(1, "float32"), "g128": _sb(1, "float32"), "n128": _sb(1, "float32"),
+    "base": _sb(1, "float32"), "j16": _sb(8, "int32"), "jcol": _sb(8, "float32"), "njcol": _sb(8, "float32"),
+    "st": _sb(16, "int32"), "Soff": _sb(16, "uint16"), "iw": _sb(1024, "float32"), "W01": _sb(16, "bfloat16"),
     "Lf": _sb(256, "bfloat16"), "eq": _sb(2048, "bfloat16"), "sc": _sb(1024, "bfloat16"), "moff": _sb(8, "uint16"),
     "mk": _sb(128, "bfloat16"), "cum": _sb(128, "bfloat16"), "le": _sb(128, "bfloat16"), "fs": _sb(64, "bfloat16"),
     "Fmsg": _sb(1, "uint16"), "Fland": _sb(7, "uint16"), "Frep": _sb(8, "uint16"), "Fdup": _sb(14, "uint16"),
@@ -67,22 +67,30 @@ def rank_program(g, core, T, topo):
     def D(q, s, out, in_):
         return inc(queues[q].dma_start(out, in_), s, 16)
 
-    def exchange(src, dst, width, base, sem, turn, codes):
+    peers = [T.cores[(rank + d) % N] for d in range(1, N)]
+    ids = []
+    for to in peers:
+        rid, pnc = topo.addr(to, core)
+        ids.append(DstId(rid=rid, pnc=pnc))
+
+    def columns(src, dst, width, base, sem):
         ts = []
         for d in range(1, N):
-            to = T.cores[(rank + d) % N]
-            rid, pnc = topo.addr(to, core)
-            eng = topo.engines(core, to)
-            a = (d - 1) * width
-            b = base + (N - d - 1) * width
+            a, b = (d - 1) * width, base + (N - d - 1) * width
             s_, d_ = T[src][:, a:a + width], T[dst][:, b:b + width]
-            if codes:
+            if src[-1] == "q":
                 s_, d_ = s_.bitcast(dt.uint8), d_.bitcast(dt.uint8)
-            ts.append(RemoteDMATransfer(dst_ids=[DstId(rid=rid, pnc=pnc)], dma_engine_mask=1 << eng[(d - 1 + turn) % len(eng)],
+            eng = topo.engines(core, peers[d - 1])
+            ts.append(RemoteDMATransfer(dst_ids=[ids[d - 1]], dma_engine_mask=1 << eng[(d - 1) % len(eng)],
                                         remote_sem=T.sem[sem], src=s_, dst=d_))
         g.remote_dma_fused(ts, local_sem=T.sem.loc)
         cnt["loc"] = cnt.get("loc", 0) + N - 1
         cnt[sem] = N - 1
+
+    def pick(out, a, win, off):
+        n = 16 * off.shape[1]
+        c = V(vec.tensor_copy(T[out + "q"][:, a:a + n].bitcast(dt.uint32), T[win + "q"][:].bitcast(dt.uint32).indirect(off)))
+        return c, A(act.activation(T[out + "s"][:, a:a + n], T[win + "s"][:].indirect(off), Act.Copy))
 
     for k in range(8):
         rows = slice(16 * k, 16 * k + 16)
@@ -95,42 +103,49 @@ def rank_program(g, core, T, topo):
     t_dv = D("s", "dv", T.vt[:], T.v[:])
 
     t_pid = G(g.iota(T.pid[:], [[0, 1]], 0, 1))
-    t_iw = G(g.iota(T.iw[:, 0:512], [[1, 512]], 0, 0, allow_small_or_imprecise_dtypes=True))
+    t_iw = G(g.iota(T.iw[:, 0:256], [[1, 256]], 0, 0, allow_small_or_imprecise_dtypes=True))
     t_j16 = G(g.iota(T.j16[:], [[16, 8]], 0, 0))
     t_w01 = G(g.iota(T.W01[:], [[1, 16]], 0, 0, allow_small_or_imprecise_dtypes=True))
     t_st = G(g.iota(T.st[:], [[16, 2], [32, 8]], 0, 0))
-    t_tab0 = V(vec.memset(T.tab[:], 0.0))
     need("v", t_pid)
     t_grp = V(vec.tensor_scalar(T.grp[:], T.pid[:], 4, None, Op.arith_shift_right))
     t_lane = V(vec.tensor_scalar(T.lane[:], T.pid[:], 15, None, Op.bitwise_and))
     need("v", t_grp)
     t_g128 = V(vec.tensor_scalar(T.g128[:], T.grp[:], 128.0, None, Op.mult))
-    t_e0 = V(vec.tensor_scalar(T.e0[:], T.grp[:], float(N - rank), None, Op.add))
+    t_n128 = V(vec.tensor_scalar(T.n128[:], T.grp[:], -128.0, None, Op.mult))
     need("v", t_lane)
     t_lanef = V(vec.tensor_copy(T.lanef[:], T.lane[:]))
-    need("v", t_e0)
-    t_e1 = V(vec.tensor_scalar(T.e1[:], T.e0[:], N - 1, None, Op.bitwise_and))
-    need("v", t_e1)
-    t_base = V(vec.tensor_scalar(T.base[:], T.e1[:], 16.0, float(S - 16 - 1), Op.mult, Op.add))
     need("v", t_iw)
-    t_iw2 = V(vec.tensor_scalar(T.iw[:, 512:1024], T.iw[:, 0:512], 512.0, None, Op.add))
+    need("a", t_iw)
+    t_iw1 = V(vec.tensor_scalar(T.iw[:, 256:512], T.iw[:, 0:256], 256.0, None, Op.add))
+    t_iw2 = A(act.activation(T.iw[:, 512:768], T.iw[:, 0:256], Act.Copy, bias=512.0))
+    t_iw3 = V(vec.tensor_scalar(T.iw[:, 768:1024], T.iw[:, 0:256], 768.0, None, Op.add))
     need("v", t_j16, t_lanef)
     t_jcol = V(vec.tensor_scalar(T.jcol[:], T.j16[:], T.lanef[:, 0:1], None, Op.add))
-    need("v", t_tab0)
-    t_own = V(vec.tensor_copy(T.tab[:, S * rank:S * rank + S], T.iw[:, 0:S]))
+    need("v", t_jcol)
+    t_njcol = V(vec.tensor_scalar(T.njcol[:], T.jcol[:], -1.0, None, Op.mult))
 
     need("v", t_dl)
     t_loff = V(vec.tensor_copy(T.Loff[:], T.L32[:]))
-    need("v", t_loff, t_iw2, t_g128)
-    t_lf = V(vec.tensor_scalar(T.Lf[:], T.iw[:].indirect(T.Loff[:]), T.g128[:, 0:1], None, Op.subtract))
-    need("v", t_lf, t_jcol)
-    t_eq = [V(vec.tensor_scalar(T.eq[:, 256 * t:256 * t + 256], T.Lf[:], T.jcol[:, t:t + 1], None, Op.is_equal)) for t in range(8)]
+    need("v", t_loff, t_iw1, t_iw2, t_iw3, t_g128)
+    need("a", t_loff, t_iw1, t_iw2, t_iw3, t_n128, t_njcol)
+    t_lf0 = V(vec.tensor_scalar(T.Lf[:, 0:S], T.iw[:].indirect(T.Loff[:, 0:8]), T.g128[:, 0:1], None, Op.subtract))
+    t_lf1 = A(act.activation(T.Lf[:, S:2 * S], T.iw[:].indirect(T.Loff[:, 8:16]), Act.Identity, bias=T.n128[:, 0:1]))
+    need("v", t_lf0, t_lf1, t_jcol)
+    need("a", t_lf0, t_lf1)
+    t_eq = []
+    for t in range(8):
+        e = T.eq[:, 256 * t:256 * t + 256]
+        if t < 5:
+            t_eq.append(V(vec.tensor_scalar(e, T.Lf[:], T.jcol[:, t:t + 1], None, Op.not_equal)))
+        else:
+            t_eq.append(A(act.activation(e, T.Lf[:], Act.Abs, bias=T.njcol[:, t:t + 1])))
     for t in range(8):
         need("v", t_eq[t])
         t_sc = V(vec.tensor_tensor_scan(T.sc[:, 128 * t:128 * t + 128], T.eq[:, 256 * t:256 * t + 128],
-                                        T.eq[:, 256 * t + 128:256 * t + 256], 0.0, Op.max, Op.max))
+                                        T.eq[:, 256 * t + 128:256 * t + 256], 1.0, Op.min, Op.min))
     need("v", t_sc)
-    t_moff = V(vec.tensor_copy(T.moff[:], T.sc[:, 127:1024:128]))
+    t_moff = V(vec.tensor_scalar(T.moff[:], T.sc[:, 127:1024:128], 0.0, None, Op.is_equal))
     need("v", t_moff, t_w01)
     t_mk = V(vec.tensor_copy(T.mk[:], T.W01[:].indirect(T.moff[:])))
     need("v", t_mk)
@@ -143,23 +158,27 @@ def rank_program(g, core, T, topo):
     t_f = V(vec.tensor_scalar(T.Fmsg[:], T.fs[:, 63:64], float(S - 1), None, Op.min))
 
     need("g", t_f)
-    ts = []
-    for d in range(1, N):
-        to = T.cores[(rank + d) % N]
-        rid, pnc = topo.addr(to, core)
-        eng = topo.engines(core, to)
-        ts.append(RemoteDMATransfer(dst_ids=[DstId(rid=rid, pnc=pnc)], dma_engine_mask=1 << eng[(d - 1) % len(eng)],
-                                    remote_sem=T.sem.arr1, src=T.Fmsg[:], dst=T.Fland[:, N - 1 - d:N - d]))
-    g.remote_dma_fused(ts, local_sem=T.sem.loc)
-    cnt["loc"] = N - 1
-    cnt["arr1"] = N - 1
+    eng = topo.engines(core, peers[0])
+    g.remote_dma_fused([RemoteDMATransfer(dst_ids=ids, dma_engine_mask=topo.mask(core, peers[0]), remote_sem=T.sem.arr1,
+                                          srcs=[T.Fmsg[:]], dsts=[T.Fland[:, N - 1 - d:N - d] for d in range(1, N)])], local_sem=T.sem.loc)
+    cnt["loc"] = len(eng)
+    cnt["arr1"] = (N - 1) * len(eng)
 
+    t_e0 = V(vec.tensor_scalar(T.e0[:], T.grp[:], float(N - rank), None, Op.add))
+    t_tab0 = V(vec.memset(T.tab[:], 0.0))
+    need("v", t_e0)
+    t_e1 = V(vec.tensor_scalar(T.e1[:], T.e0[:], N - 1, None, Op.bitwise_and))
+    need("v", t_e1)
+    t_base = V(vec.tensor_scalar(T.base[:], T.e1[:], 16.0, float(S - 16 - 1), Op.mult, Op.add))
+    need("v", t_base)
     t_tabv = V(vec.tensor_scalar(T.tabv[:], T.cum[:], T.base[:, 0:1], None, Op.add))
     for n, d in enumerate(range(1, N)):
         q = "sa"[n % 2]
         k = (rank + d) % N
-        need(q, t_tabv, t_own)
+        need(q, t_tabv)
         t_tab = D(q, "dt_", T.tab[0:128:32, S * k:S * k + S], T.tabv[16 * k:16 * k + 4, :])
+    need("v", t_tab0)
+    t_own = V(vec.tensor_copy(T.tab[:, S * rank:S * rank + S], T.iw[:, 0:S]))
     V(vec.tensor_copy(T.Ldup[:, 0:32:2], T.L32[:]))
     t_ldup = V(vec.tensor_copy(T.Ldup[:, 1:32:2], T.L32[:]))
     need("v", t_st)
@@ -167,7 +186,7 @@ def rank_program(g, core, T, topo):
     need("v", t_dx)
     t_x0 = V(vec.quantize_mx(T.x0q[:], T.x0s[:], T.xt[:]))
     t_w1 = V(vec.quantize_mx(T.W1q[:, 0:S], T.W1s[:, 0:S], T.xt[:]))
-    need("v", t_tab, t_ldup)
+    need("v", t_tab, t_ldup, t_own)
     t_p1f = V(vec.tensor_copy(T.P1f[:], T.tab[:].indirect(T.Ldup[:])))
     t_p1n = V(vec.tensor_copy(T.P1n[:], T.tab[:].indirect(T.Loff[:])))
     need("v", t_p1f)
@@ -177,23 +196,23 @@ def rank_program(g, core, T, topo):
 
     for k in range(8):
         q = "sa"[k % 2]
-        need(q, ("arr1", N - 1))
+        need(q, ("arr1", cnt["arr1"]))
         t_frep = D(q, "df", T.Frep[16 * k:16 * k + 16, 0:7], T.Fland[16 * rank:16 * rank + 16, 0:7])
     need("v", t_frep, t_x0)
-    t_s1q = V(vec.tensor_copy(T.s1q[:].bitcast(dt.uint32), T.x0q[:].bitcast(dt.uint32).indirect(T.Frep[:, 0:7])))
     need("a", t_frep, t_x0)
-    t_s1s = A(act.activation(T.s1s[:], T.x0s[:].indirect(T.Frep[:, 0:7]), Act.Copy))
-    need("g", t_s1q)
-    exchange("s1q", "W1q", 16, S, "arr2c", 0, True)
-    need("g", t_s1s)
-    exchange("s1s", "W1s", 16, S, "arr2s", N - 1, False)
+    s1c, s1s = pick("s1", 0, "x0", T.Frep[:, 0:7])
+    need("g", s1c)
+    columns("s1q", "W1q", 16, S, "arr2c")
+    need("g", s1s)
+    columns("s1s", "W1s", 16, S, "arr2s")
 
     V(vec.tensor_copy(T.Fdup[:, 0:14:2], T.Frep[:, 0:7]))
     t_fdup = V(vec.tensor_copy(T.Fdup[:, 1:14:2], T.Frep[:, 0:7]))
     need("v", t_fdup, t_p1n)
-    V(vec.tensor_copy(T.L2f[:, 0:224], T.P1n[:, 0:S].indirect(T.Fdup[:])))
-    t_l2f = V(vec.tensor_copy(T.L2f[:, 224:448], T.P1n[:, S:2 * S].indirect(T.Fdup[:])))
-    need("v", t_l2f)
+    need("a", t_fdup, t_p1n)
+    t_l2f0 = V(vec.tensor_copy(T.L2f[:, 0:224], T.P1n[:, 0:S].indirect(T.Fdup[:])))
+    t_l2f1 = A(act.activation(T.L2f[:, 224:448], T.P1n[:, S:2 * S].indirect(T.Fdup[:]), Act.Copy))
+    need("v", t_l2f0, t_l2f1)
     t_l2t = V(vec.transpose(T.L2t[:], T.L2f[:]))
     need("v", t_l2t)
     V(vec.tensor_copy(T.L2off[:, 0:14:2], T.L2t[:, 0:224:32]))
@@ -201,32 +220,23 @@ def rank_program(g, core, T, topo):
     need("v", t_da)
     V(vec.quantize_mx(T.Aq[:, 0:512], T.As[:, 0:512], T.at[:, 0:2048]))
     t_aq = V(vec.quantize_mx(T.Aq[:, 512:1024], T.As[:, 512:1024], T.at[:, 2048:4096]))
-    need("v", t_du, t_dv)
-    t_uq = V(vec.quantize_mx(T.Uq[:], T.Us[:], T.ut[:]))
-    t_vq = V(vec.quantize_mx(T.Vq[:], T.Vs[:], T.vt[:]))
 
     need("v", ("arr2c", N - 1), t_l2, t_w1)
-    t_s2q = V(vec.tensor_copy(T.s2q[:].bitcast(dt.uint32), T.W1q[:].bitcast(dt.uint32).indirect(T.L2off[:])))
     need("a", ("arr2s", N - 1), t_l2, t_w1)
-    t_s2s = A(act.activation(T.s2s[:], T.W1s[:].indirect(T.L2off[:]), Act.Copy))
-    need("g", t_s2q)
-    exchange("s2q", "L2q", 32, 0, "arr3c", 0, True)
-    need("g", t_s2s)
-    exchange("s2s", "L2s", 32, 0, "arr3s", N - 1, False)
+    s2c, s2s = pick("s2", 0, "W1", T.L2off[:])
+    need("g", s2c)
+    columns("s2q", "L2q", 32, 0, "arr3c")
+    need("g", s2s)
+    columns("s2s", "L2s", 32, 0, "arr3s")
 
+    P1 = [T.P1off[:, 0:8], T.P1off[:, 8:16]]
     need("v", t_p1)
     need("a", t_p1)
-    own_c, own_s = [], []
-    for k in range(2):
-        off = T.P1off[:, 8 * k:8 * k + 8]
-        own_c.append(V(vec.tensor_copy(T["M%dq" % k][:, 0:S].bitcast(dt.uint32), T.W1q[:].bitcast(dt.uint32).indirect(off))))
-        own_s.append(A(act.activation(T["M%ds" % k][:, 0:S], T.W1s[:].indirect(off), Act.Copy)))
+    own = [pick("M%d" % k, 0, "W1", P1[k]) for k in range(2)]
 
-    def products(ps, b, lo, hi):
-        for k in range(2):
-            w = slice(128 * (4 * k + b), 128 * (4 * k + b) + 128)
-            ins = ten.matmul_mx(ps, T.Aq[:, w], T.As[:, w], T["M%dq" % k][:, lo:hi], T["M%ds" % k][:, lo:hi], k == 0, k == 1)
-        return inc(ins, "ts")
+    def product(ps, b, k, lo, hi):
+        w = slice(128 * (4 * k + b), 128 * (4 * k + b) + 128)
+        return ten.matmul_mx(ps, T.Aq[:, w], T.As[:, w], T["M%dq" % k][:, lo:hi], T["M%ds" % k][:, lo:hi], k == 0, k == 1)
 
     def relu(q, out, ps, tok):
         need(q, tok)
@@ -234,32 +244,34 @@ def rank_program(g, core, T, topo):
             return V(vec.tensor_scalar(out, ps, 0.0, 0.05, Op.max, Op.mult))
         return A(act.activation(out, ps, Act.Relu, scale=0.05))
 
-    need("t", t_aq, *own_c, *own_s)
-    early = [products(T.psE[:, 512 * b:512 * b + S], b, 0, S) for b in range(3)]
-    hb = []
+    need("t", t_aq, *own[0], *own[1])
+    early, hb = [], []
+    for b in range(3):
+        for k in range(2):
+            ins = product(T.psE[:, 512 * b:512 * b + S], b, k, 0, S)
+        early.append(inc(ins, "ts"))
+    need("v", t_du, t_dv)
+    t_uq = V(vec.quantize_mx(T.Uq[:], T.Us[:], T.ut[:]))
+    t_vq = V(vec.quantize_mx(T.Vq[:], T.Vs[:], T.vt[:]))
     for b in range(3):
         hb.append(relu("ava"[b], T.ht[:, b:512:4], T.psE[:, 512 * b:512 * b + S], early[b]))
 
-    rem_c, rem_s = [], []
     need("v", ("arr3c", N - 1), t_soff)
     need("a", ("arr3s", N - 1), t_soff)
+    far = [pick("M%d" % k, S, "L2", T.Soff[:, 8 * k:8 * k + 7]) for k in range(2)]
+    late = {}
     for k in range(2):
-        off = T.Soff[:, 8 * k:8 * k + 7]
-        rem_c.append(V(vec.tensor_copy(T["M%dq" % k][:, S:240].bitcast(dt.uint32), T.L2q[:].bitcast(dt.uint32).indirect(off))))
-        rem_s.append(A(act.activation(T["M%ds" % k][:, S:240], T.L2s[:].indirect(off), Act.Copy)))
-    need("t", *rem_c, *rem_s)
-    late3 = products(T.ps3[:, 0:240], 3, 0, 240)
-    late = [products(T.psL[:, 512 * b:512 * b + S], b, 112, 240) for b in range(3)]
+        need("t", *far[k])
+        for b in (3, 0, 1, 2):
+            ins = product(T.ps3[:, 0:240], 3, k, 0, 240) if b == 3 else product(T.psL[:, 512 * b:512 * b + S], b, k, 112, 240)
+            if k:
+                late[b] = inc(ins, "ts")
 
-    um_c, um_s = [], []
-    need("v", *rem_c)
-    need("a", *rem_s)
-    for k in range(2):
-        off = T.P1off[:, 8 * k:8 * k + 8]
-        um_c.append(V(vec.tensor_copy(T["um%dq" % k][:].bitcast(dt.uint32), T["M%dq" % k][:].bitcast(dt.uint32).indirect(off))))
-        um_s.append(A(act.activation(T["um%ds" % k][:], T["M%ds" % k][:].indirect(off), Act.Copy)))
+    need("v", far[0][0], far[1][0])
+    need("a", far[0][1], far[1][1])
+    um = [pick("um%d" % k, 0, "M%d" % k, P1[k]) for k in range(2)]
 
-    h3 = relu("a", T.ht[:, 3:960:4], T.ps3[:, 0:240], late3)
+    h3 = relu("a", T.ht[:, 3:960:4], T.ps3[:, 0:240], late[3])
     h0 = relu("v", T.ht[:, 512:960:4], T.psL[:, 16:S], late[0])
     h1 = relu("a", T.ht[:, 513:960:4], T.psL[:, 512 + 16:512 + S], late[1])
     need("v", h3, *hb)
@@ -269,15 +281,10 @@ def rank_program(g, core, T, topo):
     t_h = V(vec.quantize_mx(T.Hq[:, 112:240], T.Hs[:, 112:240], T.ht[:, 448:960]))
     need("v", t_h)
     need("a", t_h)
-    vm_c, vm_s = [], []
-    for k in range(2):
-        off = T.P1off[:, 8 * k:8 * k + 8]
-        vm_c.append(V(vec.tensor_copy(T["vm%dq" % k][:].bitcast(dt.uint32), T.Hq[:].bitcast(dt.uint32).indirect(off))))
-        vm_s.append(A(act.activation(T["vm%ds" % k][:], T.Hs[:].indirect(off), Act.Copy)))
+    vm = [pick("vm%d" % k, 0, "H", P1[k]) for k in range(2)]
 
-    steps = [("U", "um", 0, um_c, um_s, t_uq), ("U", "um", 1, um_c, um_s, t_uq), ("V", "vm", 0, vm_c, vm_s, t_vq), ("V", "vm", 1, vm_c, vm_s, t_vq)]
-    for n, (w, m, k, c_, s_, t_) in enumerate(steps):
-        need("t", t_, c_[k], s_[k])
+    for n, (w, m, k, src, tok) in enumerate((("U", "um", 0, um, t_uq), ("U", "um", 1, um, t_uq), ("V", "vm", 0, vm, t_vq), ("V", "vm", 1, vm, t_vq))):
+        need("t", tok, *src[k])
         ks = slice(128 * k, 128 * k + 128)
         ins = ten.matmul_mx(T.psY[:, 0:S], T[w + "q"][:, ks], T[w + "s"][:, ks], T["%s%dq" % (m, k)][:], T["%s%ds" % (m, k)][:], n == 0, n == 3)
     t_y = inc(ins, "ts")

from concourse.bass import DstId, RemoteDMATransfer
from concourse.mybir import dt, AluOpType as Op, ActivationFunctionType as Act

CODE = "float8_e4m3fn_x4"


def _sb(n, d):
    return ("sbuf", [128, n], d)


SCRATCH = {
    "L32": _sb(16, "int32"), "Loff": _sb(16, "uint16"), "Ldup": _sb(32, "uint16"),
    "pid": _sb(1, "int32"), "grp": _sb(1, "int32"), "e0": _sb(1, "int32"), "e1": _sb(1, "int32"),
    "lane": _sb(1, "int32"), "lanef": _sb(1, "float32"), "g128": _sb(1, "float32"), "n128": _sb(1, "float32"),
    "base": _sb(1, "float32"), "j16": _sb(8, "int32"), "jcol": _sb(8, "float32"), "njcol": _sb(8, "float32"),
    "st": _sb(16, "int32"), "Soff": _sb(16, "uint16"), "iw": _sb(1024, "float32"), "W01": _sb(16, "bfloat16"),
    "Lf": _sb(256, "bfloat16"), "eq": _sb(2048, "bfloat16"), "sc": _sb(1024, "bfloat16"), "moff": _sb(8, "uint16"),
    "mk": _sb(128, "bfloat16"), "cum": _sb(128, "bfloat16"), "le": _sb(128, "bfloat16"), "fs": _sb(64, "bfloat16"),
    "Fmsg": _sb(1, "uint16"), "Fland": _sb(7, "uint16"), "Frep": _sb(8, "uint16"), "Fdup": _sb(14, "uint16"),
    "tabv": _sb(128, "bfloat16"), "tab": _sb(1024, "bfloat16"),
    "P1f": _sb(512, "bfloat16"), "P1t": _sb(512, "bfloat16"), "P1off": _sb(16, "uint16"), "P1n": _sb(256, "bfloat16"),
    "L2f": _sb(448, "bfloat16"), "L2t": _sb(448, "bfloat16"), "L2off": _sb(14, "uint16"),
    "xt": _sb(512, "bfloat16"), "at": _sb(4096, "bfloat16"), "vt": _sb(1024, "bfloat16"), "ut": _sb(1024, "bfloat16"),
    "ht": _sb(960, "bfloat16"), "yt": _sb(128, "float32"),
    "psE": ("psum", [128, 1536], "float32"), "psL": ("psum", [128, 1536], "float32"),
    "ps3": ("psum", [128, 512], "float32"), "psY": ("psum", [128, 512], "float32"),
}
for _n, _w in (("A", 1024), ("V", 256), ("U", 256), ("x0", 128), ("W1", 240), ("s1", 112), ("s2", 224), ("L2", 224),
               ("M0", 240), ("M1", 240), ("um0", 128), ("um1", 128), ("H", 240), ("vm0", 128), ("vm1", 128)):
    SCRATCH[_n + "q"] = _sb(_w, CODE)
    SCRATCH[_n + "s"] = _sb(_w, "uint8")

SEMAPHORES = ["vs", "as_", "ts", "gs", "dl", "dx", "da", "dv", "du", "dt_", "df", "dy",
              "arr1", "arr2c", "arr2s", "arr3c", "arr3s", "loc"]


def rank_program(g, core, T, topo):
    rank = T.rank_of(core)
    if rank is None:
        return
    N = len(T.cores)
    S = 128
    vec, act, ten, syn = g.vector, g.scalar, g.tensor, g.sync
    queues = {"g": g, "v": vec, "a": act, "t": ten, "s": syn}
    cnt, seen = {}, {}

    def inc(ins, s, n=1):
        ins.then_inc(T.sem[s], n)
        cnt[s] = cnt.get(s, 0) + n
        return (s, cnt[s])

    def need(q, *toks):
        for s, n in toks:
            if seen.get((q, s), 0) < n:
                queues[q].wait_ge(T.sem[s], n)
                seen[(q, s)] = n

    def V(ins):
        return inc(ins, "vs")

    def A(ins):
        return inc(ins, "as_")

    def G(ins):
        return inc(ins, "gs")

    def D(q, s, out, in_):
        return inc(queues[q].dma_start(out, in_), s, 16)

    peers = [T.cores[(rank + d) % N] for d in range(1, N)]
    ids = []
    for to in peers:
        rid, pnc = topo.addr(to, core)
        ids.append(DstId(rid=rid, pnc=pnc))

    def columns(src, dst, width, base, sem):
        ts = []
        for d in range(1, N):
            a, b = (d - 1) * width, base + (N - d - 1) * width
            s_, d_ = T[src][:, a:a + width], T[dst][:, b:b + width]
            if src[-1] == "q":
                s_, d_ = s_.bitcast(dt.uint8), d_.bitcast(dt.uint8)
            eng = topo.engines(core, peers[d - 1])
            ts.append(RemoteDMATransfer(dst_ids=[ids[d - 1]], dma_engine_mask=1 << eng[(d - 1) % len(eng)],
                                        remote_sem=T.sem[sem], src=s_, dst=d_))
        g.remote_dma_fused(ts, local_sem=T.sem.loc)
        cnt["loc"] = cnt.get("loc", 0) + N - 1
        cnt[sem] = N - 1

    def pick(out, a, win, off):
        n = 16 * off.shape[1]
        c = V(vec.tensor_copy(T[out + "q"][:, a:a + n].bitcast(dt.uint32), T[win + "q"][:].bitcast(dt.uint32).indirect(off)))
        return c, A(act.activation(T[out + "s"][:, a:a + n], T[win + "s"][:].indirect(off), Act.Copy))

    for k in range(8):
        rows = slice(16 * k, 16 * k + 16)
        D("s", "dl", T.L32[rows, 0:8], T.nb0[:])
        t_dl = D("a", "dl", T.L32[rows, 8:16], T.nb1[:])
    t_dx = D("s", "dx", T.xt[:], T.x[:])
    D("a", "da", T.at[:, 0:2048], T.a[:, 0:2048])
    t_da = D("s", "da", T.at[:, 2048:4096], T.a[:, 2048:4096])
    t_du = D("a", "du", T.ut[:], T.u[:])
    t_dv = D("s", "dv", T.vt[:], T.v[:])

    t_pid = G(g.iota(T.pid[:], [[0, 1]], 0, 1))
    t_iw = G(g.iota(T.iw[:, 0:256], [[1, 256]], 0, 0, allow_small_or_imprecise_dtypes=True))
    t_j16 = G(g.iota(T.j16[:], [[16, 8]], 0, 0))
    t_w01 = G(g.iota(T.W01[:], [[1, 16]], 0, 0, allow_small_or_imprecise_dtypes=True))
    t_st = G(g.iota(T.st[:], [[16, 2], [32, 8]], 0, 0))
    need("v", t_pid)
    t_grp = V(vec.tensor_scalar(T.grp[:], T.pid[:], 4, None, Op.arith_shift_right))
    t_lane = V(vec.tensor_scalar(T.lane[:], T.pid[:], 15, None, Op.bitwise_and))
    need("v", t_grp)
    t_g128 = V(vec.tensor_scalar(T.g128[:], T.grp[:], 128.0, None, Op.mult))
    t_n128 = V(vec.tensor_scalar(T.n128[:], T.grp[:], -128.0, None, Op.mult))
    need("v", t_lane)
    t_lanef = V(vec.tensor_copy(T.lanef[:], T.lane[:]))
    need("v", t_iw)
    need("a", t_iw)
    t_iw1 = V(vec.tensor_scalar(T.iw[:, 256:512], T.iw[:, 0:256], 256.0, None, Op.add))
    t_iw2 = A(act.activation(T.iw[:, 512:768], T.iw[:, 0:256], Act.Copy, bias=512.0))
    t_iw3 = V(vec.tensor_scalar(T.iw[:, 768:1024], T.iw[:, 0:256], 768.0, None, Op.add))
    need("v", t_j16, t_lanef)
    t_jcol = V(vec.tensor_scalar(T.jcol[:], T.j16[:], T.lanef[:, 0:1], None, Op.add))
    need("v", t_jcol)
    t_njcol = V(vec.tensor_scalar(T.njcol[:], T.jcol[:], -1.0, None, Op.mult))

    need("v", t_dl)
    t_loff = V(vec.tensor_copy(T.Loff[:], T.L32[:]))
    need("v", t_loff, t_iw1, t_iw2, t_iw3, t_g128)
    need("a", t_loff, t_iw1, t_iw2, t_iw3, t_n128, t_njcol)
    t_lf0 = V(vec.tensor_scalar(T.Lf[:, 0:S], T.iw[:].indirect(T.Loff[:, 0:8]), T.g128[:, 0:1], None, Op.subtract))
    t_lf1 = A(act.activation(T.Lf[:, S:2 * S], T.iw[:].indirect(T.Loff[:, 8:16]), Act.Identity, bias=T.n128[:, 0:1]))
    need("v", t_lf0, t_lf1, t_jcol)
    need("a", t_lf0, t_lf1)
    t_eq = []
    for t in range(8):
        e = T.eq[:, 256 * t:256 * t + 256]
        if t < 5:
            t_eq.append(V(vec.tensor_scalar(e, T.Lf[:], T.jcol[:, t:t + 1], None, Op.not_equal)))
        else:
            t_eq.append(A(act.activation(e, T.Lf[:], Act.Abs, bias=T.njcol[:, t:t + 1])))
    for t in range(8):
        need("v", t_eq[t])
        t_sc = V(vec.tensor_tensor_scan(T.sc[:, 128 * t:128 * t + 128], T.eq[:, 256 * t:256 * t + 128],
                                        T.eq[:, 256 * t + 128:256 * t + 256], 1.0, Op.min, Op.min))
    need("v", t_sc)
    t_moff = V(vec.tensor_scalar(T.moff[:], T.sc[:, 127:1024:128], 0.0, None, Op.is_equal))
    need("v", t_moff, t_w01)
    t_mk = V(vec.tensor_copy(T.mk[:], T.W01[:].indirect(T.moff[:])))
    need("v", t_mk)
    t_cum = V(vec.tensor_tensor_scan(T.cum[:], T.mk[:], T.mk[:], 0.0, Op.add, Op.max))
    need("v", t_cum)
    t_le = V(vec.tensor_scalar(T.le[:], T.cum[:], T.lanef[:, 0:1], None, Op.is_le))
    need("v", t_le)
    t_fs = V(vec.tensor_tensor_scan(T.fs[:], T.le[:, 0:64], T.le[:, 64:128], 0.0, Op.add, Op.add))
    need("v", t_fs)
    t_f = V(vec.tensor_scalar(T.Fmsg[:], T.fs[:, 63:64], float(S - 1), None, Op.min))

    need("g", t_f)
    eng = topo.engines(core, peers[0])
    g.remote_dma_fused([RemoteDMATransfer(dst_ids=ids, dma_engine_mask=topo.mask(core, peers[0]), remote_sem=T.sem.arr1,
                                          srcs=[T.Fmsg[:]], dsts=[T.Fland[:, N - 1 - d:N - d] for d in range(1, N)])], local_sem=T.sem.loc)
    cnt["loc"] = len(eng)
    cnt["arr1"] = (N - 1) * len(eng)

    t_e0 = V(vec.tensor_scalar(T.e0[:], T.grp[:], float(N - rank), None, Op.add))
    t_tab0 = V(vec.memset(T.tab[:], 0.0))
    need("v", t_e0)
    t_e1 = V(vec.tensor_scalar(T.e1[:], T.e0[:], N - 1, None, Op.bitwise_and))
    need("v", t_e1)
    t_base = V(vec.tensor_scalar(T.base[:], T.e1[:], 16.0, float(S - 16 - 1), Op.mult, Op.add))
    need("v", t_base)
    t_tabv = V(vec.tensor_scalar(T.tabv[:], T.cum[:], T.base[:, 0:1], None, Op.add))
    for n, d in enumerate(range(1, N)):
        q = "sa"[n % 2]
        k = (rank + d) % N
        need(q, t_tabv)
        t_tab = D(q, "dt_", T.tab[0:128:32, S * k:S * k + S], T.tabv[16 * k:16 * k + 4, :])
    need("v", t_tab0)
    t_own = V(vec.tensor_copy(T.tab[:, S * rank:S * rank + S], T.iw[:, 0:S]))
    V(vec.tensor_copy(T.Ldup[:, 0:32:2], T.L32[:]))
    t_ldup = V(vec.tensor_copy(T.Ldup[:, 1:32:2], T.L32[:]))
    need("v", t_st)
    t_soff = V(vec.tensor_scalar(T.Soff[:], T.st[:], T.lanef[:, 0:1], None, Op.add))
    need("v", t_dx)
    t_x0 = V(vec.quantize_mx(T.x0q[:], T.x0s[:], T.xt[:]))
    t_w1 = V(vec.quantize_mx(T.W1q[:, 0:S], T.W1s[:, 0:S], T.xt[:]))
    need("v", t_tab, t_ldup, t_own)
    t_p1f = V(vec.tensor_copy(T.P1f[:], T.tab[:].indirect(T.Ldup[:])))
    t_p1n = V(vec.tensor_copy(T.P1n[:], T.tab[:].indirect(T.Loff[:])))
    need("v", t_p1f)
    t_p1t = V(vec.transpose(T.P1t[:], T.P1f[:]))
    need("v", t_p1t)
    t_p1 = V(vec.tensor_copy(T.P1off[:], T.P1t[:, 0:512:32]))

    for k in range(8):
        q = "sa"[k % 2]
        need(q, ("arr1", cnt["arr1"]))
        t_frep = D(q, "df", T.Frep[16 * k:16 * k + 16, 0:7], T.Fland[16 * rank:16 * rank + 16, 0:7])
    need("v", t_frep, t_x0)
    need("a", t_frep, t_x0)
    s1c, s1s = pick("s1", 0, "x0", T.Frep[:, 0:7])
    need("g", s1c)
    columns("s1q", "W1q", 16, S, "arr2c")
    need("g", s1s)
    columns("s1s", "W1s", 16, S, "arr2s")

    V(vec.tensor_copy(T.Fdup[:, 0:14:2], T.Frep[:, 0:7]))
    t_fdup = V(vec.tensor_copy(T.Fdup[:, 1:14:2], T.Frep[:, 0:7]))
    need("v", t_fdup, t_p1n)
    need("a", t_fdup, t_p1n)
    t_l2f0 = V(vec.tensor_copy(T.L2f[:, 0:224], T.P1n[:, 0:S].indirect(T.Fdup[:])))
    t_l2f1 = A(act.activation(T.L2f[:, 224:448], T.P1n[:, S:2 * S].indirect(T.Fdup[:]), Act.Copy))
    need("v", t_l2f0, t_l2f1)
    t_l2t = V(vec.transpose(T.L2t[:], T.L2f[:]))
    need("v", t_l2t)
    V(vec.tensor_copy(T.L2off[:, 0:14:2], T.L2t[:, 0:224:32]))
    t_l2 = V(vec.tensor_copy(T.L2off[:, 1:14:2], T.L2t[:, 224:448:32]))
    need("v", t_da)
    V(vec.quantize_mx(T.Aq[:, 0:512], T.As[:, 0:512], T.at[:, 0:2048]))
    t_aq = V(vec.quantize_mx(T.Aq[:, 512:1024], T.As[:, 512:1024], T.at[:, 2048:4096]))

    need("v", ("arr2c", N - 1), t_l2, t_w1)
    need("a", ("arr2s", N - 1), t_l2, t_w1)
    s2c, s2s = pick("s2", 0, "W1", T.L2off[:])
    need("g", s2c)
    columns("s2q", "L2q", 32, 0, "arr3c")
    need("g", s2s)
    columns("s2s", "L2s", 32, 0, "arr3s")

    P1 = [T.P1off[:, 0:8], T.P1off[:, 8:16]]
    need("v", t_p1)
    need("a", t_p1)
    own = [pick("M%d" % k, 0, "W1", P1[k]) for k in range(2)]

    def product(ps, b, k, lo, hi):
        w = slice(128 * (4 * k + b), 128 * (4 * k + b) + 128)
        return ten.matmul_mx(ps, T.Aq[:, w], T.As[:, w], T["M%dq" % k][:, lo:hi], T["M%ds" % k][:, lo:hi], k == 0, k == 1)

    def relu(q, out, ps, tok):
        need(q, tok)
        if q == "v":
            return V(vec.tensor_scalar(out, ps, 0.0, 0.05, Op.max, Op.mult))
        return A(act.activation(out, ps, Act.Relu, scale=0.05))

    need("t", t_aq, *own[0], *own[1])
    early, hb = [], []
    for b in range(3):
        for k in range(2):
            ins = product(T.psE[:, 512 * b:512 * b + S], b, k, 0, S)
        early.append(inc(ins, "ts"))
    need("v", t_du, t_dv)
    t_uq = V(vec.quantize_mx(T.Uq[:], T.Us[:], T.ut[:]))
    t_vq = V(vec.quantize_mx(T.Vq[:], T.Vs[:], T.vt[:]))
    for b in range(3):
        hb.append(relu("ava"[b], T.ht[:, b:512:4], T.psE[:, 512 * b:512 * b + S], early[b]))

    need("v", ("arr3c", N - 1), t_soff)
    need("a", ("arr3s", N - 1), t_soff)
    far = [pick("M%d" % k, S, "L2", T.Soff[:, 8 * k:8 * k + 7]) for k in range(2)]
    late = {}
    for k in range(2):
        need("t", *far[k])
        for b in (3, 0, 1, 2):
            ins = product(T.ps3[:, 0:240], 3, k, 0, 240) if b == 3 else product(T.psL[:, 512 * b:512 * b + S], b, k, 112, 240)
            if k:
                late[b] = inc(ins, "ts")

    need("v", far[0][0], far[1][0])
    need("a", far[0][1], far[1][1])
    um = [pick("um%d" % k, 0, "M%d" % k, P1[k]) for k in range(2)]

    h3 = relu("a", T.ht[:, 3:960:4], T.ps3[:, 0:240], late[3])
    h0 = relu("v", T.ht[:, 512:960:4], T.psL[:, 16:S], late[0])
    h1 = relu("a", T.ht[:, 513:960:4], T.psL[:, 512 + 16:512 + S], late[1])
    need("v", h3, *hb)
    t_h_own = V(vec.quantize_mx(T.Hq[:, 0:S], T.Hs[:, 0:S], T.ht[:, 0:512]))
    h2 = relu("v", T.ht[:, 514:960:4], T.psL[:, 1024 + 16:1024 + S], late[2])
    need("v", t_h_own, h0, h1, h2)
    t_h = V(vec.quantize_mx(T.Hq[:, 112:240], T.Hs[:, 112:240], T.ht[:, 448:960]))
    need("v", t_h)
    need("a", t_h)
    vm = [pick("vm%d" % k, 0, "H", P1[k]) for k in range(2)]

    for n, (w, m, k, src, tok) in enumerate((("U", "um", 0, um, t_uq), ("U", "um", 1, um, t_uq), ("V", "vm", 0, vm, t_vq), ("V", "vm", 1, vm, t_vq))):
        need("t", tok, *src[k])
        ks = slice(128 * k, 128 * k + 128)
        ins = ten.matmul_mx(T.psY[:, 0:S], T[w + "q"][:, ks], T[w + "s"][:, ks], T["%s%dq" % (m, k)][:], T["%s%ds" % (m, k)][:], n == 0, n == 3)
    t_y = inc(ins, "ts")
    need("v", t_y)
    t_yt = V(vec.tensor_copy(T.yt[:], T.psY[:, 0:S]))
    need("s", t_yt)
    D("s", "dy", T.y[:], T.yt[:])

    for s in SEMAPHORES:
        need("g", (s, cnt[s]))
